import numpy as np
import ml_dtypes


def mxq(x, axis, fmt="e4m3"):
    dtype, down = {"e4m3": (ml_dtypes.float8_e4m3fn, 7), "e5m2": (ml_dtypes.float8_e5m2, 14)}[fmt]
    v = np.moveaxis(np.asarray(x, np.float32).astype(ml_dtypes.bfloat16).astype(np.float64), axis, -1)
    blocks = v.reshape(v.shape[:-1] + (-1, 32))
    amax = np.abs(blocks).max(-1, keepdims=True)
    byte = np.maximum(np.where(amax > 0, np.frexp(amax)[1] - 1 + 127, 0) - down, 1)
    scale = np.exp2(byte - 127.0)
    codes = (blocks / scale).astype(np.float32).astype(dtype).astype(np.float64)
    return np.moveaxis((codes * scale).reshape(v.shape), -1, axis)


WIDE = False


def mx_kscale(k):
    if not WIDE:
        return np.ones(k)
    levels = np.array([10, -10, 5, -5, 0])
    if k % 512:
        return np.exp2(np.random.permutation(np.resize(levels, k // 32))).repeat(32)
    a = np.empty((k // 512, 16))
    for p in range(k // 512):
        a[p, :8] = np.random.permutation(np.resize(levels, 8))
        for g in range(8):
            far = levels[np.abs(levels - a[p, g]) >= 10]
            a[p, g + 8] = far[np.random.randint(len(far))]
    return np.exp2(a.ravel()).repeat(32)


def f64(x):
    return np.asarray(x).astype(np.float64)


def striped(idx):
    return np.tile(idx.reshape(-1, 16).T, (8, 1)).astype(np.uint16)


def unstriped(offs):
    return offs[:16].T.reshape(-1).astype(np.int64)


E2M1 = np.array([0.0, 0.5, 1.0, 1.5, 2.0, 3.0, 4.0, 6.0, -0.0, -0.5, -1.0, -1.5, -2.0, -3.0, -4.0, -6.0])


def pack_weight(w, fmt):
    k, n = w.shape
    w = f64(np.asarray(w, np.float32).astype(ml_dtypes.bfloat16)).reshape(k // 32, 32, n)
    amax = np.abs(w).max(1)
    if fmt == "e4m3":
        byte = np.frexp(amax)[1] - 1 + 127 - 7
    else:
        mant, ex = np.frexp(amax / 6.0)
        byte = np.where(mant > 0.5, ex, ex - 1) + 127
    byte = np.clip(np.where(amax > 0, byte, 1), 1, 254)
    scaled = (w * np.exp2(127.0 - byte)[:, None, :]).reshape(k, n).astype(np.float32)
    by_word = np.ascontiguousarray(scaled.reshape(k // 512, 128, 4, n).transpose(0, 1, 3, 2))
    if fmt == "e4m3":
        words = by_word.astype(ml_dtypes.float8_e4m3fn).view(np.uint8)
    else:
        c = by_word.astype(ml_dtypes.float4_e2m1fn).view(np.uint8) & 0xF
        words = (c[..., 0::2] | (c[..., 1::2] << 4)).reshape(k // 512, 128, 2 * n)
    return np.ascontiguousarray(words), np.ascontiguousarray(byte.astype(np.uint8).reshape(k // 512, 16, n))


def unpack_weight(words, scales, fmt):
    g, _, n = scales.shape
    words = np.ascontiguousarray(words).reshape(g, 128, n, -1)
    if fmt == "e4m3":
        vals = words.view(ml_dtypes.float8_e4m3fn).astype(np.float64)
    else:
        nib = np.empty((g, 128, n, 4), np.uint8)
        nib[..., 0::2] = words & 0xF
        nib[..., 1::2] = words >> 4
        vals = E2M1[nib]
    vals = vals * np.repeat(np.exp2(scales.astype(np.float64) - 127.0), 8, axis=1)[..., None]
    return vals.transpose(0, 1, 3, 2).reshape(g * 512, n)


def gelu(v):
    return 0.5 * v * (1.0 + np.tanh(np.sqrt(2.0 / np.pi) * (v + 0.044715 * v**3)))


def bf(x):
    return np.asarray(x, np.float32).astype(ml_dtypes.bfloat16)


def planes(Y):
    n, m = Y.shape
    b = f64(bf(Y)).reshape(n // 32, 32, m)
    amax = np.abs(b).max(1)
    byte = np.clip(np.where(amax > 0, np.frexp(amax)[1] - 1 + 127 - 7, 1), 1, 254)
    codes = (b * np.exp2(127.0 - byte)[:, None, :]).reshape(n, m).astype(np.float32).astype(ml_dtypes.float8_e4m3fn).view(np.uint8)
    words = codes.reshape(n // 512, 128, 4, m).transpose(0, 1, 3, 2)
    return np.ascontiguousarray(words), np.ascontiguousarray(byte.astype(np.uint8).reshape(n // 512, 16, m))


K, H, N, T, S, T2, P = 1024, 1024, 512, 2048, 512, 1024, 512

def setup_inputs():
    n = np.random.standard_normal
    s = mx_kscale(K)[:, None]
    u = mx_kscale(H)[:, None]
    tab_words, tab_scales = pack_weight(n((K, T)) * s, "e4m3")
    w1 = 1.3 * n((K, H)) * K ** -0.5 / s
    w2_words, w2_scales = pack_weight(0.5 * n((K, H)) * K ** -0.5 / s, "e2m1")
    w3_words, w3_scales = pack_weight(n((H, N)) * H ** -0.5 / u * np.exp(0.8 * n(N))[None, :], "e4m3")
    sign = np.where(n(H) > 0, 1.0, -1.0)
    return {
        "tab_words": tab_words, "tab_scales": tab_scales,
        "offs": striped(np.random.permutation(T)[:S]),
        "offs2": striped(np.random.permutation(T2)[:S]),
        "offs3": striped(np.random.permutation(T2)[:P]),
        "w1": w1.astype(np.float32),
        "w2_words": w2_words, "w2_scales": w2_scales,
        "bias": (0.3 * n(H) - 0.4).astype(np.float32),
        "wgs": np.exp(0.3 * n((128, S))).astype(np.float32),
        "page0": (0.8 * n((H, T2))).astype(np.float32),
        "base": (P * np.random.uniform(0.05, 0.15, H)).astype(np.float32),
        "gain": (P * np.random.uniform(0.8, 2.2, H) * sign * u[:, 0]).astype(np.float32),
        "plan": (0.6 * n((H, P)) * u).astype(np.float32),
        "w3_words": w3_words, "w3_scales": w3_scales,
    }

def reference(tab_words, tab_scales, offs, offs2, offs3, w1, w2_words, w2_scales, bias, wgs, page0, base, gain, plan, w3_words, w3_scales):
    v = unpack_weight(tab_words, tab_scales, "e4m3")[:, unstriped(offs)]
    flow = mxq(f64(w1), 0, "e4m3").T @ v
    delay = unpack_weight(w2_words, w2_scales, "e2m1").T @ v
    h = np.tanh(flow) + np.abs(delay) + f64(bias)[:, None]
    page = f64(page0).copy()
    page[:, unstriped(offs2)] = np.tile(f64(wgs), (H // 128, 1)) * h
    top = page.max(axis=1)
    a = np.exp(page[:, unstriped(offs3)] - top[:, None])
    share = f64(gain) / (f64(base) + a.sum(axis=1))
    m = share[:, None] * a + f64(plan)
    y = unpack_weight(w3_words, w3_scales, "e4m3").T @ mxq(m, 0, "e4m3")
    words, scales = planes(y)
    return y, words, scales

@@ -1,0 +1,352 @@
+from contextlib import ExitStack
+
+import concourse.mybir as mybir
+
+K, H, N, T, S, T2, M = 1024, 1024, 512, 2048, 512, 1024, 512
+FLOPS = 2 * (2 * K * H * S + H * N * M)
+
+F32 = mybir.dt.float32
+BF16 = mybir.dt.bfloat16
+I32 = mybir.dt.int32
+U32 = mybir.dt.uint32
+U16 = mybir.dt.uint16
+U8 = mybir.dt.uint8
+FP8X4 = mybir.dt.float8_e4m3fn_x4
+FP4X4 = mybir.dt.float4_e2m1fn_x4
+ACT = mybir.ActivationFunctionType
+ALU = mybir.AluOpType
+AX = mybir.AxisListType
+
+P = 128
+QW = 128
+
+
+def tile_list_shuttle_congestion_map_kernel(
+    tc, tab_words, tab_scales, offs, offs2, offs3, w1, w2_words, w2_scales, bias, wgs, page0,
+    base, gain, plan, w3_words, w3_scales, out_0, out_1, out_2,
+):
+    nc = tc.nc
+    with ExitStack() as ctx:
+        keep = ctx.enter_context(tc.tile_pool(name="keep", bufs=1))
+        ring = ctx.enter_context(tc.tile_pool(name="ring", bufs=3))
+        psum = ctx.enter_context(tc.psum_pool(name="psum", bufs=1))
+
+        def sb(name, shape, dtype):
+            return keep.tile(shape, dtype, name=name, align_bytes=64)
+
+        idx = sb("idx", [P, S // 16], U16)
+        idx2 = sb("idx2", [P, S // 16], U16)
+        idx3 = sb("idx3", [P, M // 16], U16)
+        tab_sc = sb("tab_sc", [P, 2 * T], U8)
+        w2_sc = sb("w2_sc", [P, 2 * H], U8)
+        w3_sc = sb("w3_sc", [P, 2 * N], U8)
+        tab_w = [sb("tab_w%d" % a, [P, T], I32) for a in range(2)]
+        w1_raw = [[sb("w1_raw%d%d" % (b, a), [P, 4, 512], F32) for a in range(2)] for b in range(2)]
+        w1_bf = [[None, None], [None, None]]
+        w1_q = [[sb("w1_q0%d" % a, [P, 512], U32) for a in range(2)], [None, None]]
+        w1_s = [[sb("w1_s%d%d" % (b, a), [P, 512], U8) for a in range(2)] for b in range(2)]
+        w2_raw = [sb("w2_raw%d" % b, [P, 2, 1024], U8) for b in range(2)]
+        w2_q = [sb("w2_q%d" % b, [P, 2, 1024], U8) for b in range(2)]
+        w2_s = sb("w2_s", [P, 4, 512], U8)
+        w3_raw = sb("w3_raw", [P, 2, N], I32)
+        w3_q = sb("w3_q", [P, 2, N], U32)
+        w3_s = sb("w3_s", [P, 2, N], U8)
+        v_q = [sb("v_q%d" % a, [P, S], U32) for a in range(2)]
+        v_s = [sb("v_s%d" % a, [P, S], U8) for a in range(2)]
+        bias_t = sb("bias_t", [P, 2, 8], F32)
+        base_t = sb("base_t", [P, 2, 8], F32)
+        gain_t = sb("gain_t", [P, 2, 8], F32)
+        wgs_t = sb("wgs_t", [P, 4, S], F32)
+        pages = [sb("page%d" % u, [P, T2], F32) for u in range(8)]
+        plan_t = [sb("plan%d" % b, [P, 4, M], F32) for b in range(2)]
+        looks = [sb("look%d" % u, [P, M], F32) for u in range(8)]
+        d_pl = [sb("d_pl%d" % b, [P, 4, M], BF16) for b in range(2)]
+        d_bf = [sb("d_bf%d" % b, [P, 4 * M], BF16) for b in range(2)]
+        d_q = [sb("d_q%d" % b, [P, M], U32) for b in range(2)]
+        d_s = [sb("d_s%d" % b, [P, M], U8) for b in range(2)]
+        y_f = sb("y_f", [P, 4, M], F32)
+        y_bf = sb("y_bf", [P, 4 * M], BF16)
+        y_q = sb("y_q", [P, M], I32)
+        y_s = sb("y_s", [P, M], U8)
+        y_ps = [psum.tile([P, 4, QW], F32, name="y_ps%d" % q) for q in range(4)]
+
+        def load_scales(queue, tile, dram):
+            for q in range(4):
+                queue.dma_start(
+                    out=tile[32 * q : 32 * q + 4, :].bitcast(I32).rearrange("p (a n) -> p a n", a=2),
+                    in_=dram[:, 4 * q : 4 * q + 4, :].bitcast(I32).rearrange("a r n -> r a n"),
+                )
+
+        def load_w1(b, a):
+            nc.sync.dma_start(
+                out=w1_raw[b][a][:],
+                in_=w1[512 * a : 512 * (a + 1), 512 * b : 512 * (b + 1)].rearrange("(p j) c -> p j c", j=4),
+            )
+
+        def load_w2(b):
+            nc.sync.dma_start(
+                out=w2_raw[b][:].bitcast(I32),
+                in_=w2_words[:, :, 1024 * b : 1024 * (b + 1)].bitcast(I32).rearrange("a p n -> p a n"),
+            )
+
+        page_rows = page0.rearrange("(b p i) c -> b i p c", b=2, i=4)
+        plan_rows = plan.rearrange("(b p i) m -> b p i m", b=2, i=4)
+
+        def load_page(u):
+            nc.sync.dma_start(out=pages[u][:], in_=page_rows[u // 4, u % 4])
+
+        def load_vec(tile, dram):
+            nc.sync.dma_start(out=tile[:, :, 0:4], in_=dram.rearrange("(b p i) -> p b i", b=2, i=4))
+
+        def cast_w1(b, a):
+            w1_bf[b][a] = keep.tile([P, 2048], BF16, name="w1_bf%d%d" % (b, a), tag="w1_bf%d" % a, align_bytes=64)
+            nc.scalar.copy(
+                out=w1_bf[b][a][:].rearrange("p (i m j) -> p m j i", i=4, j=4),
+                in_=w1_raw[b][a][:].rearrange("p j (m i) -> p m j i", i=4),
+            )
+
+        def quant_w1(b, a):
+            if b == 1:
+                w1_q[b][a] = keep.tile([P, 512], U32, name="w1_q1%d" % a, tag="h%d" % (a + 1), align_bytes=64)
+            nc.vector.quantize_mx(out=w1_q[b][a][:].bitcast(FP8X4), scales=w1_s[b][a][:], in_=w1_bf[b][a][:])
+
+        def deal_w2(b):
+            nc.scalar.copy(
+                out=w2_q[b][:].bitcast(U16).rearrange("p a (i m) -> p a i m", i=4),
+                in_=w2_raw[b][:].bitcast(U16).rearrange("p a (m i) -> p a i m", i=4),
+            )
+
+        def deal_w2_scales():
+            nc.vector.tensor_copy(
+                out=w2_s[:].rearrange("p g (i m) -> p g i m", i=4),
+                in_=w2_sc[:].rearrange("p (g m i) -> p g i m", g=4, i=4),
+            )
+
+        def deal_w3():
+            nc.scalar.copy(
+                out=w3_q[:].rearrange("p a (t m) -> p a m t", t=4),
+                in_=w3_raw[:].bitcast(U32).rearrange("p a (m t) -> p a m t", t=4),
+            )
+            nc.vector.tensor_copy(
+                out=w3_s[:].rearrange("p a (t m) -> p a t m", t=4),
+                in_=w3_sc[:].rearrange("p (a m t) -> p a t m", a=2, t=4),
+            )
+
+        acts = {}
+
+        def first_stage(u, j0=0, j1=S):
+            b, i = divmod(u, 4)
+            cols = slice(P * i, P * (i + 1))
+            js = slice(j0, j1)
+            flow = psum.tile([P, j1 - j0], F32, name="flow", bufs=2)
+            delay = psum.tile([P, j1 - j0], F32, name="delay", bufs=2)
+            for a in range(2):
+                nc.tensor.matmul_mx(
+                    out=flow[:], lhsT=w1_q[b][a][:, cols].bitcast(FP8X4), lhsT_scale=w1_s[b][a][:, cols],
+                    rhs=v_q[a][:, js].bitcast(FP8X4), rhs_scale=v_s[a][:, js], start=(a == 0), stop=(a == 1),
+                )
+            for a in range(2):
+                nc.tensor.matmul_mx(
+                    out=delay[:], lhsT=w2_q[b][:, a, 2 * P * i : 2 * P * (i + 1)].bitcast(FP4X4),
+                    lhsT_scale=w2_s[:, 2 * a + b, cols],
+                    rhs=v_q[a][:, js].bitcast(FP8X4), rhs_scale=v_s[a][:, js], start=(a == 0), stop=(a == 1),
+                )
+            th = ring.tile([P, j1 - j0], F32, name="th")
+            ab = ring.tile([P, j1 - j0], F32, name="ab")
+            nc.scalar.activation(out=th[:], in_=flow[:], func=ACT.Tanh)
+            nc.scalar.activation(out=ab[:], in_=delay[:], func=ACT.Abs)
+            acts.setdefault(u, []).append((j0, j1, th, ab))
+
+        ntops = {}
+
+        def put(u):
+            b, i = divmod(u, 4)
+            h = keep.tile([P, S], F32, name="h%d" % u, tag="h%d" % (u if u in (1, 2) else 3 + u % 2), align_bytes=64)
+            for j0, j1, th, ab in acts[u]:
+                nc.vector.scalar_tensor_tensor(
+                    out=h[:, j0:j1], in0=ab[:], scalar=bias_t[:, b, i : i + 1], in1=th[:], op0=ALU.add, op1=ALU.add
+                )
+                nc.vector.tensor_tensor(
+                    out=pages[u][:].indirect(idx2[:, j0 // 16 : j1 // 16]), in0=h[:, j0:j1],
+                    in1=wgs_t[:, i, j0:j1], op=ALU.mult,
+                )
+            ntop = ring.tile([P, 1], F32, name="ntop")
+            nc.vector.reduce_max(out=ntop[:], in_=pages[u][:], axis=AX.X, negate=True)
+            ntops[u] = ntop
+
+        dens = sb("dens", [P, 8], F32)
+
+        def look(u):
+            b, i = divmod(u, 4)
+            nc.scalar.activation(out=looks[u][:], in_=pages[u][:].indirect(idx3[:]), func=ACT.Exp, bias=ntops[u][:])
+            echo = ring.tile([P, M], BF16, name="echo")
+            total = ring.tile([P, 1], F32, name="total")
+            nc.scalar.activation(out=echo[:], in_=looks[u][:], func=ACT.Copy, accum_out=total[:])
+            nc.scalar.activation(out=dens[:, u : u + 1], in_=total[:], func=ACT.Identity, bias=base_t[:, b, i : i + 1])
+
+        def mix(u0, u1):
+            b, i0 = divmod(u0, 4)
+            n = u1 - u0
+            rec = ring.tile([P, n], F32, name="rec")
+            share = ring.tile([P, n], F32, name="share")
+            nc.vector.reciprocal(out=rec[:], in_=dens[:, u0:u1])
+            nc.vector.tensor_tensor(out=share[:], in0=rec[:], in1=gain_t[:, b, i0 : i0 + n], op=ALU.mult)
+            for e in range(n):
+                nc.vector.scalar_tensor_tensor(
+                    out=d_pl[b][:, i0 + e, :], in0=looks[u0 + e][:], scalar=share[:, e : e + 1],
+                    in1=plan_t[b][:, i0 + e, :], op0=ALU.mult, op1=ALU.add,
+                )
+
+        def last_tile(u):
+            b, i = divmod(u, 4)
+            parts = ring.tile([P, 2], F32, name="parts")
+            echo = ring.tile([P, M], BF16, name="echo")
+            start = base_t[:, b, i : i + 1]
+            for e in range(2):
+                mc = slice(M // 2 * e, M // 2 * (e + 1))
+                nc.scalar.activation(
+                    out=looks[u][:, mc], in_=pages[u][:].indirect(idx3[:, M // 32 * e : M // 32 * (e + 1)]),
+                    func=ACT.Exp, bias=ntops[u][:],
+                )
+                nc.vector.tensor_scalar(
+                    out=echo[:, mc], in0=looks[u][:, mc], scalar1=1.0, scalar2=start, op0=ALU.mult, op1=ALU.add,
+                    accum_out=parts[:, e : e + 1],
+                )
+                start = parts[:, e : e + 1]
+            rec = ring.tile([P, 1], F32, name="rec")
+            share = ring.tile([P, 1], F32, name="share")
+            nc.vector.reciprocal(out=rec[:], in_=start)
+            nc.vector.tensor_tensor(out=share[:], in0=rec[:], in1=gain_t[:, b, i : i + 1], op=ALU.mult)
+            return share
+
+        def weave(engine_copy, b, c0, c1):
+            engine_copy(
+                out=d_bf[b][:, 4 * c0 : 4 * c1].rearrange("p (c e i) -> p c i e", e=4, i=4),
+                in_=d_pl[b][:, :, c0:c1].rearrange("p i (c e) -> p c i e", e=4),
+            )
+
+        def quant_d(b, c0, c1):
+            nc.vector.quantize_mx(
+                out=d_q[b][:, c0:c1].bitcast(FP8X4), scales=d_s[b][:, c0:c1], in_=d_bf[b][:, 4 * c0 : 4 * c1]
+            )
+
+        def second_stage(b, q):
+            mc = slice(QW * q, QW * (q + 1))
+            for t in range(4):
+                nt = slice(P * t, P * (t + 1))
+                nc.tensor.matmul_mx(
+                    out=y_ps[q][:, t, :], lhsT=w3_q[:, b, nt].bitcast(FP8X4), lhsT_scale=w3_s[:, b, nt],
+                    rhs=d_q[b][:, mc].bitcast(FP8X4), rhs_scale=d_s[b][:, mc],
+                    start=(b == 0 and t == 0), stop=(b == 1 and t == 3),
+                )
+
+        nc.vector.memset(tab_sc[:].bitcast(I32), 0)
+        nc.gpsimd.memset(w2_sc[:].bitcast(I32), 0)
+        nc.gpsimd.memset(w3_sc[:].bitcast(I32), 0)
+        nc.sync.dma_start(out=idx[:], in_=offs)
+        nc.sync.dma_start(out=idx2[:], in_=offs2)
+        nc.sync.dma_start(out=idx3[:], in_=offs3)
+        load_vec(bias_t, bias)
+        load_scales(nc.scalar, tab_sc, tab_scales)
+        load_scales(nc.gpsimd, w2_sc, w2_scales)
+        load_w1(0, 0)
+        load_w1(0, 1)
+        load_w2(0)
+        for a in range(2):
+            nc.sync.dma_start(out=tab_w[a][:], in_=tab_words[a].rearrange("p t i -> p (t i)").bitcast(I32))
+        load_page(0)
+        wgs_rows = wgs.rearrange("(p i) j -> p i j", i=4)
+        for q in (0, 2, 1, 3):
+            nc.sync.dma_start(out=wgs_t[32 * q : 32 * (q + 1)], in_=wgs_rows)
+        load_w1(1, 0)
+        load_w1(1, 1)
+        load_page(1)
+        load_w2(1)
+        load_vec(base_t, base)
+        load_vec(gain_t, gain)
+        load_page(2)
+        load_page(3)
+        load_page(4)
+        nc.sync.dma_start(
+            out=w3_raw[:], in_=w3_words.rearrange("a p n t -> p a (n t)").bitcast(I32)
+        )
+        load_scales(nc.sync, w3_sc, w3_scales)
+        nc.sync.dma_start(out=plan_t[0][:], in_=plan_rows[0])
+        load_page(5)
+        load_page(6)
+        load_page(7)
+        nc.sync.dma_start(out=plan_t[1][:], in_=plan_rows[1])
+
+        cast_w1(0, 0)
+        cast_w1(0, 1)
+        deal_w2(0)
+        for a in range(2):
+            nc.vector.tensor_copy(out=v_s[a][:], in_=tab_sc[:, T * a : T * (a + 1)].indirect(idx[:]))
+        deal_w2_scales()
+        quant_w1(0, 0)
+        nc.vector.tensor_copy(out=v_q[0][:], in_=tab_w[0][:].bitcast(U32).indirect(idx[:]))
+        quant_w1(0, 1)
+        for j0 in (0, S // 2):
+            j1 = j0 + S // 2
+            nc.vector.tensor_copy(
+                out=v_q[1][:, j0:j1], in_=tab_w[1][:].bitcast(U32).indirect(idx[:, j0 // 16 : j1 // 16])
+            )
+            first_stage(0, j0, j1)
+
+        first_stage(1)
+        for u in range(8):
+            put(u)
+            if u + 2 < 8:
+                if u == 0:
+                    cast_w1(1, 0)
+                    cast_w1(1, 1)
+                    deal_w2(1)
+                if u == 1:
+                    quant_w1(1, 0)
+                if u == 2:
+                    quant_w1(1, 1)
+                first_stage(u + 2)
+            if u < 7:
+                look(u)
+            if u == 4:
+                mix(0, 4)
+                deal_w3()
+                weave(nc.scalar.copy, 0, 0, M)
+            if u == 5:
+                quant_d(0, 0, M)
+                for q in range(4):
+                    second_stage(0, q)
+        mix(4, 7)
+        share = last_tile(7)
+        y_rows = out_0.rearrange("(p t) m -> p t m", t=4)
+        words = out_1[0].rearrange("p m t -> p (m t)").bitcast(I32)
+        for step in range(6):
+            if step < 4:
+                mc = slice(QW * step, QW * (step + 1))
+                nc.vector.scalar_tensor_tensor(
+                    out=d_pl[1][:, 3, mc], in0=looks[7][:, mc], scalar=share[:], in1=plan_t[1][:, 3, mc],
+                    op0=ALU.mult, op1=ALU.add,
+                )
+            if 1 <= step < 5:
+                weave(nc.vector.tensor_copy, 1, QW * (step - 1), QW * step)
+            if step >= 2:
+                quant_d(1, QW * (step - 2), QW * (step - 1))
+                second_stage(1, step - 2)
+        for q in range(4):
+            mc = slice(QW * q, QW * (q + 1))
+            nc.scalar.copy(out=y_f[:, :, mc], in_=y_ps[q][:])
+            nc.vector.tensor_copy(
+                out=y_bf[:, 4 * QW * q : 4 * QW * (q + 1)].rearrange("p (c e t) -> p c t e", e=4, t=4),
+                in_=y_f[:, :, mc].rearrange("p t (c e) -> p c t e", e=4),
+            )
+            if q % 2 == 1:
+                hc = slice(QW * (q - 1), QW * (q + 1))
+                nc.sync.dma_start(out=y_rows[:, :, hc], in_=y_f[:, :, hc])
+                nc.vector.quantize_mx(
+                    out=y_q[:, hc].bitcast(FP8X4), scales=y_s[:, hc], in_=y_bf[:, 4 * QW * (q - 1) : 4 * QW * (q + 1)]
+                )
+                nc.sync.dma_start(out=words[:, hc], in_=y_q[:, hc])
+        for q in range(4):
+            nc.scalar.dma_start(
+                out=out_2[0, 4 * q : 4 * q + 4, :].bitcast(I32), in_=y_s[32 * q : 32 * q + 4, :].bitcast(I32)
+            )

@@ -1,6 +1,7 @@
 from contextlib import ExitStack
 
 import concourse.mybir as mybir
+from concourse.masks import make_identity
 
 K, H, N, T, S, T2, M = 1024, 1024, 512, 2048, 512, 1024, 512
 FLOPS = 2 * (2 * K * H * S + H * N * M)
@@ -41,13 +42,12 @@ def tile_list_shuttle_congestion_map_kernel(
         w2_sc = sb("w2_sc", [P, 2 * H], U8)
         w3_sc = sb("w3_sc", [P, 2 * N], U8)
         tab_w = [sb("tab_w%d" % a, [P, T], I32) for a in range(2)]
+        ident = sb("ident", [P, P], F32)
         w1_raw = [[sb("w1_raw%d%d" % (b, a), [P, 4, 512], F32) for a in range(2)] for b in range(2)]
         w1_bf = [[None, None], [None, None]]
         w1_q = [[sb("w1_q0%d" % a, [P, 512], U32) for a in range(2)], [None, None]]
         w1_s = [[sb("w1_s%d%d" % (b, a), [P, 512], U8) for a in range(2)] for b in range(2)]
         w2_raw = [sb("w2_raw%d" % b, [P, 2, 1024], U8) for b in range(2)]
-        w2_q = [sb("w2_q%d" % b, [P, 2, 1024], U8) for b in range(2)]
-        w2_s = sb("w2_s", [P, 4, 512], U8)
         w3_raw = sb("w3_raw", [P, 2, N], I32)
         w3_q = sb("w3_q", [P, 2, N], U32)
         w3_s = sb("w3_s", [P, 2, N], U8)
@@ -56,10 +56,10 @@ def tile_list_shuttle_congestion_map_kernel(
         bias_t = sb("bias_t", [P, 2, 8], F32)
         base_t = sb("base_t", [P, 2, 8], F32)
         gain_t = sb("gain_t", [P, 2, 8], F32)
-        wgs_t = sb("wgs_t", [P, 4, S], F32)
+        wgs_t = [sb("wgs_t%d" % half, [P, 2, S], F32) for half in range(2)]
         pages = [sb("page%d" % u, [P, T2], F32) for u in range(8)]
         plan_t = [sb("plan%d" % b, [P, 4, M], F32) for b in range(2)]
-        looks = [sb("look%d" % u, [P, M], F32) for u in range(8)]
+        looks = {u: sb("look%d" % u, [P, M], F32)[:] for u in range(4, 8)}
         d_pl = [sb("d_pl%d" % b, [P, 4, M], BF16) for b in range(2)]
         d_bf = [sb("d_bf%d" % b, [P, 4 * M], BF16) for b in range(2)]
         d_q = [sb("d_q%d" % b, [P, M], U32) for b in range(2)]
@@ -68,7 +68,7 @@ def tile_list_shuttle_congestion_map_kernel(
         y_bf = sb("y_bf", [P, 4 * M], BF16)
         y_q = sb("y_q", [P, M], I32)
         y_s = sb("y_s", [P, M], U8)
-        y_ps = [psum.tile([P, 4, QW], F32, name="y_ps%d" % q) for q in range(4)]
+        y_ps = []
 
         def load_scales(queue, tile, dram):
             for q in range(4):
@@ -101,26 +101,14 @@ def tile_list_shuttle_congestion_map_kernel(
         def cast_w1(b, a):
             w1_bf[b][a] = keep.tile([P, 2048], BF16, name="w1_bf%d%d" % (b, a), tag="w1_bf%d" % a, align_bytes=64)
             nc.scalar.copy(
-                out=w1_bf[b][a][:].rearrange("p (i m j) -> p m j i", i=4, j=4),
-                in_=w1_raw[b][a][:].rearrange("p j (m i) -> p m j i", i=4),
+                out=w1_bf[b][a][:].rearrange("p (c e j) -> p c j e", e=4, j=4),
+                in_=w1_raw[b][a][:].rearrange("p j (c e) -> p c j e", e=4),
             )
 
         def quant_w1(b, a):
             if b == 1:
                 w1_q[b][a] = keep.tile([P, 512], U32, name="w1_q1%d" % a, tag="h%d" % (a + 1), align_bytes=64)
             nc.vector.quantize_mx(out=w1_q[b][a][:].bitcast(FP8X4), scales=w1_s[b][a][:], in_=w1_bf[b][a][:])
-
-        def deal_w2(b):
-            nc.scalar.copy(
-                out=w2_q[b][:].bitcast(U16).rearrange("p a (i m) -> p a i m", i=4),
-                in_=w2_raw[b][:].bitcast(U16).rearrange("p a (m i) -> p a i m", i=4),
-            )
-
-        def deal_w2_scales():
-            nc.vector.tensor_copy(
-                out=w2_s[:].rearrange("p g (i m) -> p g i m", i=4),
-                in_=w2_sc[:].rearrange("p (g m i) -> p g i m", g=4, i=4),
-            )
 
         def deal_w3():
             nc.scalar.copy(
@@ -132,92 +120,110 @@ def tile_list_shuttle_congestion_map_kernel(
                 in_=w3_sc[:].rearrange("p (a m t) -> p a t m", a=2, t=4),
             )
 
-        acts = {}
+        th = [None, None]
+        ab = [None, None]
 
-        def first_stage(u, j0=0, j1=S):
-            b, i = divmod(u, 4)
-            cols = slice(P * i, P * (i + 1))
-            js = slice(j0, j1)
-            flow = psum.tile([P, j1 - j0], F32, name="flow", bufs=2)
-            delay = psum.tile([P, j1 - j0], F32, name="delay", bufs=2)
+        def open_group(b):
+            tags = ("th0", "ab0") if b == 0 else ("tab_w0", "tab_w1")
+            th[b] = keep.tile([P, 4, 4, P], F32, name="th%d" % b, tag=tags[0], align_bytes=64)
+            ab[b] = keep.tile([P, 4, 4, P], F32, name="ab%d" % b, tag=tags[1], align_bytes=64)
+
+        def first_stage(b, jt):
+            js = slice(P * jt, P * (jt + 1))
+            flow = psum.tile([P, 512], F32, name="flow", bufs=3)
+            delay = psum.tile([P, 512], F32, name="delay", bufs=3)
             for a in range(2):
                 nc.tensor.matmul_mx(
-                    out=flow[:], lhsT=w1_q[b][a][:, cols].bitcast(FP8X4), lhsT_scale=w1_s[b][a][:, cols],
-                    rhs=v_q[a][:, js].bitcast(FP8X4), rhs_scale=v_s[a][:, js], start=(a == 0), stop=(a == 1),
+                    out=flow[:], lhsT=v_q[a][:, js].bitcast(FP8X4), lhsT_scale=v_s[a][:, js],
+                    rhs=w1_q[b][a][:].bitcast(FP8X4), rhs_scale=w1_s[b][a][:], start=(a == 0), stop=(a == 1),
                 )
             for a in range(2):
                 nc.tensor.matmul_mx(
-                    out=delay[:], lhsT=w2_q[b][:, a, 2 * P * i : 2 * P * (i + 1)].bitcast(FP4X4),
-                    lhsT_scale=w2_s[:, 2 * a + b, cols],
-                    rhs=v_q[a][:, js].bitcast(FP8X4), rhs_scale=v_s[a][:, js], start=(a == 0), stop=(a == 1),
+                    out=delay[:], lhsT=v_q[a][:, js].bitcast(FP8X4), lhsT_scale=v_s[a][:, js],
+                    rhs=w2_raw[b][:, a, :].bitcast(FP4X4),
+                    rhs_scale=w2_sc[:, H * a + 512 * b : H * a + 512 * (b + 1)], start=(a == 0), stop=(a == 1),
                 )
-            th = ring.tile([P, j1 - j0], F32, name="th")
-            ab = ring.tile([P, j1 - j0], F32, name="ab")
-            nc.scalar.activation(out=th[:], in_=flow[:], func=ACT.Tanh)
-            nc.scalar.activation(out=ab[:], in_=delay[:], func=ACT.Abs)
-            acts.setdefault(u, []).append((j0, j1, th, ab))
+            nc.scalar.activation(out=th[b][:, jt], in_=flow[:].rearrange("j (p i) -> j i p", i=4), func=ACT.Tanh)
+            nc.scalar.activation(out=ab[b][:, jt], in_=delay[:].rearrange("j (p i) -> j i p", i=4), func=ACT.Abs)
 
+        hs = {}
         ntops = {}
 
-        def put(u):
+        def open_h(u):
+            tag = {1: "h1", 2: "h2", 6: "w1_raw11", 7: "d_pl0"}.get(u, "h_ring%d" % (u % 3))
+            hs[u] = keep.tile([P, S], F32, name="h%d" % u, tag=tag, align_bytes=64)
+
+        def turn(pieces):
+            bank = psum.tile([P, len(pieces), P], F32, name="hsum", bufs=2)
+            for n, (u, jt) in enumerate(pieces):
+                b, i = divmod(u, 4)
+                for term, first in ((th[b], True), (ab[b], False)):
+                    nc.tensor.matmul(
+                        out=bank[:, n, :], lhsT=term[:, jt, i, :], rhs=ident[:], is_transpose=True,
+                        start=first, stop=not first,
+                    )
+            return bank
+
+        def settle(u, j0, j1, src):
             b, i = divmod(u, 4)
-            h = keep.tile([P, S], F32, name="h%d" % u, tag="h%d" % (u if u in (1, 2) else 3 + u % 2), align_bytes=64)
-            for j0, j1, th, ab in acts[u]:
-                nc.vector.scalar_tensor_tensor(
-                    out=h[:, j0:j1], in0=ab[:], scalar=bias_t[:, b, i : i + 1], in1=th[:], op0=ALU.add, op1=ALU.add
-                )
-                nc.vector.tensor_tensor(
-                    out=pages[u][:].indirect(idx2[:, j0 // 16 : j1 // 16]), in0=h[:, j0:j1],
-                    in1=wgs_t[:, i, j0:j1], op=ALU.mult,
-                )
-            ntop = ring.tile([P, 1], F32, name="ntop")
+            nc.scalar.activation(out=hs[u][:, j0:j1], in_=src, func=ACT.Identity, bias=bias_t[:, b, i : i + 1])
+
+        def put(u, j0, j1):
+            i = u % 4
+            nc.vector.tensor_tensor(
+                out=pages[u][:].indirect(idx2[:, j0 // 16 : j1 // 16]), in0=hs[u][:, j0:j1],
+                in1=wgs_t[i // 2][:, i % 2, j0:j1], op=ALU.mult,
+            )
+
+        def peak(u):
+            ntop = keep.tile([P, 1], F32, name="ntop%d" % u)
             nc.vector.reduce_max(out=ntop[:], in_=pages[u][:], axis=AX.X, negate=True)
             ntops[u] = ntop
+
+        def sliced_pair(b, before_slice):
+            us = (4 * b, 4 * b + 1)
+            for u in us:
+                open_h(u)
+            for jt in range(4):
+                before_slice(jt)
+                first_stage(b, jt)
+                bank = turn([(u, jt) for u in us])
+                for n, u in enumerate(us):
+                    settle(u, P * jt, P * (jt + 1), bank[:, n, :])
+                    put(u, P * jt, P * (jt + 1))
+
+        def whole_tile(u):
+            open_h(u)
+            bank = turn([(u, jt) for jt in range(4)])
+            settle(u, 0, S, bank[:].rearrange("p n j -> p (n j)"))
 
         dens = sb("dens", [P, 8], F32)
 
         def look(u):
             b, i = divmod(u, 4)
-            nc.scalar.activation(out=looks[u][:], in_=pages[u][:].indirect(idx3[:]), func=ACT.Exp, bias=ntops[u][:])
+            nc.scalar.activation(out=looks[u], in_=pages[u][:].indirect(idx3[:]), func=ACT.Exp, bias=ntops[u][:])
             echo = ring.tile([P, M], BF16, name="echo")
             total = ring.tile([P, 1], F32, name="total")
-            nc.scalar.activation(out=echo[:], in_=looks[u][:], func=ACT.Copy, accum_out=total[:])
+            nc.scalar.activation(out=echo[:], in_=looks[u], func=ACT.Copy, accum_out=total[:])
             nc.scalar.activation(out=dens[:, u : u + 1], in_=total[:], func=ACT.Identity, bias=base_t[:, b, i : i + 1])
 
-        def mix(u0, u1):
+        def shares(u0, u1):
             b, i0 = divmod(u0, 4)
             n = u1 - u0
             rec = ring.tile([P, n], F32, name="rec")
             share = ring.tile([P, n], F32, name="share")
             nc.vector.reciprocal(out=rec[:], in_=dens[:, u0:u1])
             nc.vector.tensor_tensor(out=share[:], in0=rec[:], in1=gain_t[:, b, i0 : i0 + n], op=ALU.mult)
-            for e in range(n):
+            return share
+
+        def mix(u0, u1):
+            b, i0 = divmod(u0, 4)
+            share = shares(u0, u1)
+            for e in range(u1 - u0):
                 nc.vector.scalar_tensor_tensor(
-                    out=d_pl[b][:, i0 + e, :], in0=looks[u0 + e][:], scalar=share[:, e : e + 1],
+                    out=d_pl[b][:, i0 + e, :], in0=looks[u0 + e], scalar=share[:, e : e + 1],
                     in1=plan_t[b][:, i0 + e, :], op0=ALU.mult, op1=ALU.add,
                 )
-
-        def last_tile(u):
-            b, i = divmod(u, 4)
-            parts = ring.tile([P, 2], F32, name="parts")
-            echo = ring.tile([P, M], BF16, name="echo")
-            start = base_t[:, b, i : i + 1]
-            for e in range(2):
-                mc = slice(M // 2 * e, M // 2 * (e + 1))
-                nc.scalar.activation(
-                    out=looks[u][:, mc], in_=pages[u][:].indirect(idx3[:, M // 32 * e : M // 32 * (e + 1)]),
-                    func=ACT.Exp, bias=ntops[u][:],
-                )
-                nc.vector.tensor_scalar(
-                    out=echo[:, mc], in0=looks[u][:, mc], scalar1=1.0, scalar2=start, op0=ALU.mult, op1=ALU.add,
-                    accum_out=parts[:, e : e + 1],
-                )
-                start = parts[:, e : e + 1]
-            rec = ring.tile([P, 1], F32, name="rec")
-            share = ring.tile([P, 1], F32, name="share")
-            nc.vector.reciprocal(out=rec[:], in_=start)
-            nc.vector.tensor_tensor(out=share[:], in0=rec[:], in1=gain_t[:, b, i : i + 1], op=ALU.mult)
-            return share
 
         def weave(engine_copy, b, c0, c1):
             engine_copy(
@@ -240,84 +246,106 @@ def tile_list_shuttle_congestion_map_kernel(
                     start=(b == 0 and t == 0), stop=(b == 1 and t == 3),
                 )
 
+        wgs_rows = wgs.rearrange("(p i) j -> p i j", i=4)
+
+        def load_wgs(half):
+            for q in (0, 2, 1, 3):
+                nc.sync.dma_start(out=wgs_t[half][32 * q : 32 * (q + 1)], in_=wgs_rows[:, 2 * half : 2 * half + 2])
+
         nc.vector.memset(tab_sc[:].bitcast(I32), 0)
         nc.gpsimd.memset(w2_sc[:].bitcast(I32), 0)
+        load_scales(nc.gpsimd, w2_sc, w2_scales)
         nc.gpsimd.memset(w3_sc[:].bitcast(I32), 0)
+        make_identity(nc, ident[:])
         nc.sync.dma_start(out=idx[:], in_=offs)
         nc.sync.dma_start(out=idx2[:], in_=offs2)
         nc.sync.dma_start(out=idx3[:], in_=offs3)
         load_vec(bias_t, bias)
         load_scales(nc.scalar, tab_sc, tab_scales)
-        load_scales(nc.gpsimd, w2_sc, w2_scales)
         load_w1(0, 0)
         load_w1(0, 1)
         load_w2(0)
         for a in range(2):
             nc.sync.dma_start(out=tab_w[a][:], in_=tab_words[a].rearrange("p t i -> p (t i)").bitcast(I32))
+        load_wgs(0)
         load_page(0)
-        wgs_rows = wgs.rearrange("(p i) j -> p i j", i=4)
-        for q in (0, 2, 1, 3):
-            nc.sync.dma_start(out=wgs_t[32 * q : 32 * (q + 1)], in_=wgs_rows)
+        load_page(1)
         load_w1(1, 0)
         load_w1(1, 1)
-        load_page(1)
+        load_wgs(1)
+        load_page(2)
         load_w2(1)
+        load_page(3)
         load_vec(base_t, base)
         load_vec(gain_t, gain)
-        load_page(2)
-        load_page(3)
         load_page(4)
+        load_page(5)
         nc.sync.dma_start(
             out=w3_raw[:], in_=w3_words.rearrange("a p n t -> p a (n t)").bitcast(I32)
         )
         load_scales(nc.sync, w3_sc, w3_scales)
         nc.sync.dma_start(out=plan_t[0][:], in_=plan_rows[0])
-        load_page(5)
         load_page(6)
         load_page(7)
         nc.sync.dma_start(out=plan_t[1][:], in_=plan_rows[1])
 
         cast_w1(0, 0)
         cast_w1(0, 1)
-        deal_w2(0)
         for a in range(2):
             nc.vector.tensor_copy(out=v_s[a][:], in_=tab_sc[:, T * a : T * (a + 1)].indirect(idx[:]))
-        deal_w2_scales()
         quant_w1(0, 0)
         nc.vector.tensor_copy(out=v_q[0][:], in_=tab_w[0][:].bitcast(U32).indirect(idx[:]))
         quant_w1(0, 1)
-        for j0 in (0, S // 2):
-            j1 = j0 + S // 2
-            nc.vector.tensor_copy(
-                out=v_q[1][:, j0:j1], in_=tab_w[1][:].bitcast(U32).indirect(idx[:, j0 // 16 : j1 // 16])
-            )
-            first_stage(0, j0, j1)
 
-        first_stage(1)
-        for u in range(8):
-            put(u)
-            if u + 2 < 8:
-                if u == 0:
-                    cast_w1(1, 0)
-                    cast_w1(1, 1)
-                    deal_w2(1)
-                if u == 1:
-                    quant_w1(1, 0)
-                if u == 2:
-                    quant_w1(1, 1)
-                first_stage(u + 2)
-            if u < 7:
-                look(u)
-            if u == 4:
-                mix(0, 4)
-                deal_w3()
-                weave(nc.scalar.copy, 0, 0, M)
-            if u == 5:
-                quant_d(0, 0, M)
-                for q in range(4):
-                    second_stage(0, q)
+        def fetch_words(jt):
+            nc.vector.tensor_copy(
+                out=v_q[1][:, P * jt : P * (jt + 1)],
+                in_=tab_w[1][:].bitcast(U32).indirect(idx[:, 8 * jt : 8 * (jt + 1)]),
+            )
+
+        open_group(0)
+        sliced_pair(0, fetch_words)
+        cast_w1(1, 0)
+        whole_tile(2)
+        peak(0)
+        peak(1)
+        quant_w1(1, 0)
+        cast_w1(1, 1)
+        whole_tile(3)
+        put(2, 0, S)
+        quant_w1(1, 1)
+        peak(2)
+        put(3, 0, S)
+        peak(3)
+        open_group(1)
+        sliced_pair(1, lambda jt: None)
+        for a in range(2):
+            pair = keep.tile([P, 2, M], F32, name="look_pair%d" % a, tag="w1_raw1%d" % (1 - a), align_bytes=64)
+            for e in range(2):
+                looks[2 * a + e] = pair[:, e, :]
+        for u in range(4):
+            look(u)
+        peak(4)
+        peak(5)
+        mix(0, 4)
+        whole_tile(6)
+        deal_w3()
+        weave(nc.scalar.copy, 0, 0, M)
+        whole_tile(7)
+        look(4)
+        look(5)
+        put(6, 0, S)
+        peak(6)
+        quant_d(0, 0, M)
+        for q in range(4):
+            y_ps.append(psum.tile([P, 4, QW], F32, name="y_ps%d" % q, tag=("flow", "delay")[q % 2], bufs=3))
+            second_stage(0, q)
+        look(6)
+        put(7, 0, S)
+        peak(7)
+        look(7)
         mix(4, 7)
-        share = last_tile(7)
+        share = shares(7, 8)
         y_rows = out_0.rearrange("(p t) m -> p t m", t=4)
         words = out_1[0].rearrange("p m t -> p (m t)").bitcast(I32)
         for step in range(6):
@@ -328,7 +356,7 @@ def tile_list_shuttle_congestion_map_kernel(
                     op0=ALU.mult, op1=ALU.add,
                 )
             if 1 <= step < 5:
-                weave(nc.vector.tensor_copy, 1, QW * (step - 1), QW * step)
+                weave((nc.scalar.copy, nc.vector.tensor_copy)[step % 2], 1, QW * (step - 1), QW * step)
             if step >= 2:
                 quant_d(1, QW * (step - 2), QW * (step - 1))
                 second_stage(1, step - 2)

@@ -143,14 +143,19 @@ def tile_list_shuttle_congestion_map_kernel(
                     rhs=w2_raw[b][:, a, :].bitcast(FP4X4),
                     rhs_scale=w2_sc[:, H * a + 512 * b : H * a + 512 * (b + 1)], start=(a == 0), stop=(a == 1),
                 )
-            nc.scalar.activation(out=th[b][:, jt], in_=flow[:].rearrange("j (p i) -> j i p", i=4), func=ACT.Tanh)
-            nc.scalar.activation(out=ab[b][:, jt], in_=delay[:].rearrange("j (p i) -> j i p", i=4), func=ACT.Abs)
+            return flow, delay
+
+        def bend(b, jt, sums, i0, i1):
+            for term, bank, func in ((th[b], sums[0], ACT.Tanh), (ab[b], sums[1], ACT.Abs)):
+                nc.scalar.activation(
+                    out=term[:, jt, i0:i1], in_=bank[:].rearrange("j (p i) -> j i p", i=4)[:, i0:i1], func=func
+                )
 
         hs = {}
         ntops = {}
 
         def open_h(u):
-            tag = {1: "h1", 2: "h2", 6: "w1_raw11", 7: "d_pl0"}.get(u, "h_ring%d" % (u % 3))
+            tag = {1: "h1", 2: "h2"}.get(u, "h_ring%d" % (u % 3))
             hs[u] = keep.tile([P, S], F32, name="h%d" % u, tag=tag, align_bytes=64)
 
         def turn(pieces):
@@ -180,17 +185,23 @@ def tile_list_shuttle_congestion_map_kernel(
             nc.vector.reduce_max(out=ntop[:], in_=pages[u][:], axis=AX.X, negate=True)
             ntops[u] = ntop
 
-        def sliced_pair(b, before_slice):
+        def sliced_pair(b, before_slice, first_planes):
             us = (4 * b, 4 * b + 1)
             for u in us:
                 open_h(u)
+            sums = []
             for jt in range(4):
                 before_slice(jt)
-                first_stage(b, jt)
+                sums.append(first_stage(b, jt))
+                bend(b, jt, sums[jt], 0, first_planes)
                 bank = turn([(u, jt) for u in us])
+                if first_planes < 4 and jt >= 1:
+                    bend(b, jt - 1, sums[jt - 1], first_planes, 4)
                 for n, u in enumerate(us):
                     settle(u, P * jt, P * (jt + 1), bank[:, n, :])
                     put(u, P * jt, P * (jt + 1))
+            if first_planes < 4:
+                bend(b, 3, sums[3], first_planes, 4)
 
         def whole_tile(u):
             open_h(u)
@@ -304,7 +315,7 @@ def tile_list_shuttle_congestion_map_kernel(
             )
 
         open_group(0)
-        sliced_pair(0, fetch_words)
+        sliced_pair(0, fetch_words, 2)
         cast_w1(1, 0)
         whole_tile(2)
         peak(0)
@@ -318,20 +329,19 @@ def tile_list_shuttle_congestion_map_kernel(
         put(3, 0, S)
         peak(3)
         open_group(1)
-        sliced_pair(1, lambda jt: None)
-        for a in range(2):
-            pair = keep.tile([P, 2, M], F32, name="look_pair%d" % a, tag="w1_raw1%d" % (1 - a), align_bytes=64)
-            for e in range(2):
-                looks[2 * a + e] = pair[:, e, :]
+        sliced_pair(1, lambda jt: None, 4)
+        first_looks = keep.tile([P, 4, M], F32, name="first_looks", tag="w1_raw11", align_bytes=64)
+        for u in range(4):
+            looks[u] = first_looks[:, u, :]
         for u in range(4):
             look(u)
+        whole_tile(6)
         peak(4)
         peak(5)
         mix(0, 4)
-        whole_tile(6)
         deal_w3()
-        weave(nc.scalar.copy, 0, 0, M)
         whole_tile(7)
+        weave(nc.scalar.copy, 0, 0, M)
         look(4)
         look(5)
         put(6, 0, S)

@@ -268,12 +268,12 @@ def tile_list_shuttle_congestion_map_kernel(
         load_scales(nc.gpsimd, w2_sc, w2_scales)
         nc.gpsimd.memset(w3_sc[:].bitcast(I32), 0)
         make_identity(nc, ident[:])
+        load_w1(0, 0)
         nc.sync.dma_start(out=idx[:], in_=offs)
         nc.sync.dma_start(out=idx2[:], in_=offs2)
         nc.sync.dma_start(out=idx3[:], in_=offs3)
         load_vec(bias_t, bias)
         load_scales(nc.scalar, tab_sc, tab_scales)
-        load_w1(0, 0)
         load_w1(0, 1)
         load_w2(0)
         for a in range(2):

from contextlib import ExitStack

import concourse.mybir as mybir
from concourse.masks import make_identity

K, H, N, T, S, T2, M = 1024, 1024, 512, 2048, 512, 1024, 512
FLOPS = 2 * (2 * K * H * S + H * N * M)

F32 = mybir.dt.float32
BF16 = mybir.dt.bfloat16
I32 = mybir.dt.int32
U32 = mybir.dt.uint32
U16 = mybir.dt.uint16
U8 = mybir.dt.uint8
FP8X4 = mybir.dt.float8_e4m3fn_x4
FP4X4 = mybir.dt.float4_e2m1fn_x4
ACT = mybir.ActivationFunctionType
ALU = mybir.AluOpType
AX = mybir.AxisListType

P = 128
QW = 128


def tile_list_shuttle_congestion_map_kernel(
    tc, tab_words, tab_scales, offs, offs2, offs3, w1, w2_words, w2_scales, bias, wgs, page0,
    base, gain, plan, w3_words, w3_scales, out_0, out_1, out_2,
):
    nc = tc.nc
    with ExitStack() as ctx:
        keep = ctx.enter_context(tc.tile_pool(name="keep", bufs=1))
        ring = ctx.enter_context(tc.tile_pool(name="ring", bufs=3))
        psum = ctx.enter_context(tc.psum_pool(name="psum", bufs=1))

        def sb(name, shape, dtype):
            return keep.tile(shape, dtype, name=name, align_bytes=64)

        idx = sb("idx", [P, S // 16], U16)
        idx2 = sb("idx2", [P, S // 16], U16)
        idx3 = sb("idx3", [P, M // 16], U16)
        tab_sc = sb("tab_sc", [P, 2 * T], U8)
        w2_sc = sb("w2_sc", [P, 2 * H], U8)
        w3_sc = sb("w3_sc", [P, 2 * N], U8)
        tab_w = [sb("tab_w%d" % a, [P, T], I32) for a in range(2)]
        ident = sb("ident", [P, P], F32)
        w1_raw = [[sb("w1_raw%d%d" % (b, a), [P, 4, 512], F32) for a in range(2)] for b in range(2)]
        w1_bf = [[None, None], [None, None]]
        w1_q = [[sb("w1_q0%d" % a, [P, 512], U32) for a in range(2)], [None, None]]
        w1_s = [[sb("w1_s%d%d" % (b, a), [P, 512], U8) for a in range(2)] for b in range(2)]
        w2_raw = [sb("w2_raw%d" % b, [P, 2, 1024], U8) for b in range(2)]
        w3_raw = sb("w3_raw", [P, 2, N], I32)
        w3_q = sb("w3_q", [P, 2, N], U32)
        w3_s = sb("w3_s", [P, 2, N], U8)
        v_q = [sb("v_q%d" % a, [P, S], U32) for a in range(2)]
        v_s = [sb("v_s%d" % a, [P, S], U8) for a in range(2)]
        bias_t = sb("bias_t", [P, 2, 8], F32)
        base_t = sb("base_t", [P, 2, 8], F32)
        gain_t = sb("gain_t", [P, 2, 8], F32)
        wgs_t = [sb("wgs_t%d" % half, [P, 2, S], F32) for half in range(2)]
        pages = [sb("page%d" % u, [P, T2], F32) for u in range(8)]
        plan_t = [sb("plan%d" % b, [P, 4, M], F32) for b in range(2)]
        looks = {u: sb("look%d" % u, [P, M], F32)[:] for u in range(4, 8)}
        d_pl = [sb("d_pl%d" % b, [P, 4, M], BF16) for b in range(2)]
        d_bf = [sb("d_bf%d" % b, [P, 4 * M], BF16) for b in range(2)]
        d_q = [sb("d_q%d" % b, [P, M], U32) for b in range(2)]
        d_s = [sb("d_s%d" % b, [P, M], U8) for b in range(2)]
        y_f = sb("y_f", [P, 4, M], F32)
        y_bf = sb("y_bf", [P, 4 * M], BF16)
        y_q = sb("y_q", [P, M], I32)
        y_s = sb("y_s", [P, M], U8)
        y_ps = []

        def load_scales(queue, tile, dram):
            for q in range(4):
                queue.dma_start(
                    out=tile[32 * q : 32 * q + 4, :].bitcast(I32).rearrange("p (a n) -> p a n", a=2),
                    in_=dram[:, 4 * q : 4 * q + 4, :].bitcast(I32).rearrange("a r n -> r a n"),
                )

        def load_w1(b, a):
            nc.sync.dma_start(
                out=w1_raw[b][a][:],
                in_=w1[512 * a : 512 * (a + 1), 512 * b : 512 * (b + 1)].rearrange("(p j) c -> p j c", j=4),
            )

        def load_w2(b):
            nc.sync.dma_start(
                out=w2_raw[b][:].bitcast(I32),
                in_=w2_words[:, :, 1024 * b : 1024 * (b + 1)].bitcast(I32).rearrange("a p n -> p a n"),
            )

        page_rows = page0.rearrange("(b p i) c -> b i p c", b=2, i=4)
        plan_rows = plan.rearrange("(b p i) m -> b p i m", b=2, i=4)

        def load_page(u):
            nc.sync.dma_start(out=pages[u][:], in_=page_rows[u // 4, u % 4])

        def load_vec(tile, dram):
            nc.sync.dma_start(out=tile[:, :, 0:4], in_=dram.rearrange("(b p i) -> p b i", b=2, i=4))

        def cast_w1(b, a):
            w1_bf[b][a] = keep.tile([P, 2048], BF16, name="w1_bf%d%d" % (b, a), tag="w1_bf%d" % a, align_bytes=64)
            nc.scalar.copy(
                out=w1_bf[b][a][:].rearrange("p (c e j) -> p c j e", e=4, j=4),
                in_=w1_raw[b][a][:].rearrange("p j (c e) -> p c j e", e=4),
            )

        def quant_w1(b, a):
            if b == 1:
                w1_q[b][a] = keep.tile([P, 512], U32, name="w1_q1%d" % a, tag="h%d" % (a + 1), align_bytes=64)
            nc.vector.quantize_mx(out=w1_q[b][a][:].bitcast(FP8X4), scales=w1_s[b][a][:], in_=w1_bf[b][a][:])

        def deal_w3():
            nc.scalar.copy(
                out=w3_q[:].rearrange("p a (t m) -> p a m t", t=4),
                in_=w3_raw[:].bitcast(U32).rearrange("p a (m t) -> p a m t", t=4),
            )
            nc.vector.tensor_copy(
                out=w3_s[:].rearrange("p a (t m) -> p a t m", t=4),
                in_=w3_sc[:].rearrange("p (a m t) -> p a t m", a=2, t=4),
            )

        th = [None, None]
        ab = [None, None]

        def open_group(b):
            tags = ("th0", "ab0") if b == 0 else ("tab_w0", "tab_w1")
            th[b] = keep.tile([P, 4, 4, P], F32, name="th%d" % b, tag=tags[0], align_bytes=64)
            ab[b] = keep.tile([P, 4, 4, P], F32, name="ab%d" % b, tag=tags[1], align_bytes=64)

        def first_stage(b, jt):
            js = slice(P * jt, P * (jt + 1))
            flow = psum.tile([P, 512], F32, name="flow", bufs=3)
            delay = psum.tile([P, 512], F32, name="delay", bufs=3)
            for a in range(2):
                nc.tensor.matmul_mx(
                    out=flow[:], lhsT=v_q[a][:, js].bitcast(FP8X4), lhsT_scale=v_s[a][:, js],
                    rhs=w1_q[b][a][:].bitcast(FP8X4), rhs_scale=w1_s[b][a][:], start=(a == 0), stop=(a == 1),
                )
            for a in range(2):
                nc.tensor.matmul_mx(
                    out=delay[:], lhsT=v_q[a][:, js].bitcast(FP8X4), lhsT_scale=v_s[a][:, js],
                    rhs=w2_raw[b][:, a, :].bitcast(FP4X4),
                    rhs_scale=w2_sc[:, H * a + 512 * b : H * a + 512 * (b + 1)], start=(a == 0), stop=(a == 1),
                )
            return flow, delay

        def bend(b, jt, sums, i0, i1):
            for term, bank, func in ((th[b], sums[0], ACT.Tanh), (ab[b], sums[1], ACT.Abs)):
                nc.scalar.activation(
                    out=term[:, jt, i0:i1], in_=bank[:].rearrange("j (p i) -> j i p", i=4)[:, i0:i1], func=func
                )

        hs = {}
        ntops = {}

        def open_h(u):
            tag = {1: "h1", 2: "h2"}.get(u, "h_ring%d" % (u % 3))
            hs[u] = keep.tile([P, S], F32, name="h%d" % u, tag=tag, align_bytes=64)

        def turn(pieces):
            bank = psum.tile([P, len(pieces), P], F32, name="hsum", bufs=2)
            for n, (u, jt) in enumerate(pieces):
                b, i = divmod(u, 4)
                for term, first in ((th[b], True), (ab[b], False)):
                    nc.tensor.matmul(
                        out=bank[:, n, :], lhsT=term[:, jt, i, :], rhs=ident[:], is_transpose=True,
                        start=first, stop=not first,
                    )
            return bank

        def settle(u, j0, j1, src):
            b, i = divmod(u, 4)
            nc.scalar.activation(out=hs[u][:, j0:j1], in_=src, func=ACT.Identity, bias=bias_t[:, b, i : i + 1])

        def put(u, j0, j1):
            i = u % 4
            nc.vector.tensor_tensor(
                out=pages[u][:].indirect(idx2[:, j0 // 16 : j1 // 16]), in0=hs[u][:, j0:j1],
                in1=wgs_t[i // 2][:, i % 2, j0:j1], op=ALU.mult,
            )

        def peak(u):
            ntop = keep.tile([P, 1], F32, name="ntop%d" % u)
            nc.vector.reduce_max(out=ntop[:], in_=pages[u][:], axis=AX.X, negate=True)
            ntops[u] = ntop

        def sliced_pair(b, before_slice, first_planes):
            us = (4 * b, 4 * b + 1)
            for u in us:
                open_h(u)
            sums = []
            for jt in range(4):
                before_slice(jt)
                sums.append(first_stage(b, jt))
                bend(b, jt, sums[jt], 0, first_planes)
                bank = turn([(u, jt) for u in us])
                if first_planes < 4 and jt >= 1:
                    bend(b, jt - 1, sums[jt - 1], first_planes, 4)
                for n, u in enumerate(us):
                    settle(u, P * jt, P * (jt + 1), bank[:, n, :])
                    put(u, P * jt, P * (jt + 1))
            if first_planes < 4:
                bend(b, 3, sums[3], first_planes, 4)

        def whole_tile(u):
            open_h(u)
            bank = turn([(u, jt) for jt in range(4)])
            settle(u, 0, S, bank[:].rearrange("p n j -> p (n j)"))

        dens = sb("dens", [P, 8], F32)

        def look(u):
            b, i = divmod(u, 4)
            nc.scalar.activation(out=looks[u], in_=pages[u][:].indirect(idx3[:]), func=ACT.Exp, bias=ntops[u][:])
            echo = ring.tile([P, M], BF16, name="echo")
            total = ring.tile([P, 1], F32, name="total")
            nc.scalar.activation(out=echo[:], in_=looks[u], func=ACT.Copy, accum_out=total[:])
            nc.scalar.activation(out=dens[:, u : u + 1], in_=total[:], func=ACT.Identity, bias=base_t[:, b, i : i + 1])

        def shares(u0, u1):
            b, i0 = divmod(u0, 4)
            n = u1 - u0
            rec = ring.tile([P, n], F32, name="rec")
            share = ring.tile([P, n], F32, name="share")
            nc.vector.reciprocal(out=rec[:], in_=dens[:, u0:u1])
            nc.vector.tensor_tensor(out=share[:], in0=rec[:], in1=gain_t[:, b, i0 : i0 + n], op=ALU.mult)
            return share

        def mix(u0, u1):
            b, i0 = divmod(u0, 4)
            share = shares(u0, u1)
            for e in range(u1 - u0):
                nc.vector.scalar_tensor_tensor(
                    out=d_pl[b][:, i0 + e, :], in0=looks[u0 + e], scalar=share[:, e : e + 1],
                    in1=plan_t[b][:, i0 + e, :], op0=ALU.mult, op1=ALU.add,
                )

        def weave(engine_copy, b, c0, c1):
            engine_copy(
                out=d_bf[b][:, 4 * c0 : 4 * c1].rearrange("p (c e i) -> p c i e", e=4, i=4),
                in_=d_pl[b][:, :, c0:c1].rearrange("p i (c e) -> p c i e", e=4),
            )

        def quant_d(b, c0, c1):
            nc.vector.quantize_mx(
                out=d_q[b][:, c0:c1].bitcast(FP8X4), scales=d_s[b][:, c0:c1], in_=d_bf[b][:, 4 * c0 : 4 * c1]
            )

        def second_stage(b, q):
            mc = slice(QW * q, QW * (q + 1))
            for t in range(4):
                nt = slice(P * t, P * (t + 1))
                nc.tensor.matmul_mx(
                    out=y_ps[q][:, t, :], lhsT=w3_q[:, b, nt].bitcast(FP8X4), lhsT_scale=w3_s[:, b, nt],
                    rhs=d_q[b][:, mc].bitcast(FP8X4), rhs_scale=d_s[b][:, mc],
                    start=(b == 0 and t == 0), stop=(b == 1 and t == 3),
                )

        wgs_rows = wgs.rearrange("(p i) j -> p i j", i=4)

        def load_wgs(half):
            for q in (0, 2, 1, 3):
                nc.sync.dma_start(out=wgs_t[half][32 * q : 32 * (q + 1)], in_=wgs_rows[:, 2 * half : 2 * half + 2])

        nc.vector.memset(tab_sc[:].bitcast(I32), 0)
        nc.gpsimd.memset(w2_sc[:].bitcast(I32), 0)
        load_scales(nc.gpsimd, w2_sc, w2_scales)
        nc.gpsimd.memset(w3_sc[:].bitcast(I32), 0)
        make_identity(nc, ident[:])
        load_w1(0, 0)
        nc.sync.dma_start(out=idx[:], in_=offs)
        nc.sync.dma_start(out=idx2[:], in_=offs2)
        nc.sync.dma_start(out=idx3[:], in_=offs3)
        load_vec(bias_t, bias)
        load_scales(nc.scalar, tab_sc, tab_scales)
        load_w1(0, 1)
        load_w2(0)
        for a in range(2):
            nc.sync.dma_start(out=tab_w[a][:], in_=tab_words[a].rearrange("p t i -> p (t i)").bitcast(I32))
        load_wgs(0)
        load_page(0)
        load_page(1)
        load_w1(1, 0)
        load_w1(1, 1)
        load_wgs(1)
        load_page(2)
        load_w2(1)
        load_page(3)
        load_vec(base_t, base)
        load_vec(gain_t, gain)
        load_page(4)
        load_page(5)
        nc.sync.dma_start(
            out=w3_raw[:], in_=w3_words.rearrange("a p n t -> p a (n t)").bitcast(I32)
        )
        load_scales(nc.sync, w3_sc, w3_scales)
        nc.sync.dma_start(out=plan_t[0][:], in_=plan_rows[0])
        load_page(6)
        load_page(7)
        nc.sync.dma_start(out=plan_t[1][:], in_=plan_rows[1])

        cast_w1(0, 0)
        cast_w1(0, 1)
        for a in range(2):
            nc.vector.tensor_copy(out=v_s[a][:], in_=tab_sc[:, T * a : T * (a + 1)].indirect(idx[:]))
        quant_w1(0, 0)
        nc.vector.tensor_copy(out=v_q[0][:], in_=tab_w[0][:].bitcast(U32).indirect(idx[:]))
        quant_w1(0, 1)

        def fetch_words(jt):
            nc.vector.tensor_copy(
                out=v_q[1][:, P * jt : P * (jt + 1)],
                in_=tab_w[1][:].bitcast(U32).indirect(idx[:, 8 * jt : 8 * (jt + 1)]),
            )

        open_group(0)
        sliced_pair(0, fetch_words, 2)
        cast_w1(1, 0)
        whole_tile(2)
        peak(0)
        peak(1)
        quant_w1(1, 0)
        cast_w1(1, 1)
        whole_tile(3)
        put(2, 0, S)
        quant_w1(1, 1)
        peak(2)
        put(3, 0, S)
        peak(3)
        open_group(1)
        sliced_pair(1, lambda jt: None, 4)
        first_looks = keep.tile([P, 4, M], F32, name="first_looks", tag="w1_raw11", align_bytes=64)
        for u in range(4):
            looks[u] = first_looks[:, u, :]
        for u in range(4):
            look(u)
        whole_tile(6)
        peak(4)
        peak(5)
        mix(0, 4)
        deal_w3()
        whole_tile(7)
        weave(nc.scalar.copy, 0, 0, M)
        look(4)
        look(5)
        put(6, 0, S)
        peak(6)
        quant_d(0, 0, M)
        for q in range(4):
            y_ps.append(psum.tile([P, 4, QW], F32, name="y_ps%d" % q, tag=("flow", "delay")[q % 2], bufs=3))
            second_stage(0, q)
        look(6)
        put(7, 0, S)
        peak(7)
        look(7)
        mix(4, 7)
        share = shares(7, 8)
        y_rows = out_0.rearrange("(p t) m -> p t m", t=4)
        words = out_1[0].rearrange("p m t -> p (m t)").bitcast(I32)
        for step in range(6):
            if step < 4:
                mc = slice(QW * step, QW * (step + 1))
                nc.vector.scalar_tensor_tensor(
                    out=d_pl[1][:, 3, mc], in0=looks[7][:, mc], scalar=share[:], in1=plan_t[1][:, 3, mc],
                    op0=ALU.mult, op1=ALU.add,
                )
            if 1 <= step < 5:
                weave((nc.scalar.copy, nc.vector.tensor_copy)[step % 2], 1, QW * (step - 1), QW * step)
            if step >= 2:
                quant_d(1, QW * (step - 2), QW * (step - 1))
                second_stage(1, step - 2)
        for q in range(4):
            mc = slice(QW * q, QW * (q + 1))
            nc.scalar.copy(out=y_f[:, :, mc], in_=y_ps[q][:])
            nc.vector.tensor_copy(
                out=y_bf[:, 4 * QW * q : 4 * QW * (q + 1)].rearrange("p (c e t) -> p c t e", e=4, t=4),
                in_=y_f[:, :, mc].rearrange("p t (c e) -> p c t e", e=4),
            )
            if q % 2 == 1:
                hc = slice(QW * (q - 1), QW * (q + 1))
                nc.sync.dma_start(out=y_rows[:, :, hc], in_=y_f[:, :, hc])
                nc.vector.quantize_mx(
                    out=y_q[:, hc].bitcast(FP8X4), scales=y_s[:, hc], in_=y_bf[:, 4 * QW * (q - 1) : 4 * QW * (q + 1)]
                )
                nc.sync.dma_start(out=words[:, hc], in_=y_q[:, hc])
        for q in range(4):
            nc.scalar.dma_start(
                out=out_2[0, 4 * q : 4 * q + 4, :].bitcast(I32), in_=y_s[32 * q : 32 * q + 4, :].bitcast(I32)
            )
